import numpy as np, ml_dtypes
CORES = [6,15,38,47]
N = 4
BF = ml_dtypes.bfloat16
def gentries(a):
    return np.ascontiguousarray(a.reshape(8, 16, -1).transpose(0, 2, 1)).reshape(8, -1)
def gtable(e):
    e = np.asarray(e); return np.ascontiguousarray(e.reshape(8, -1, 16).transpose(0, 2, 1)).reshape(128, -1).astype(np.int32)
W, K, F, O, C, V = 4096, 640, 2, 4, 8, 250
def pick(a, ix):
    return np.take_along_axis(a, ix[:, None, :], 2)
def draw_lists(rng):
    return rng.permuted(np.tile(np.arange(W, dtype=np.int64), (N, 8, N, F, O, 1)), axis=-1)[..., :K].copy()
def frames(rng, T, L, share):
    o = rng.integers(0, O, (N, 8, N, F)); B = np.zeros((N, 8, 16, N, F, K), np.int64)
    for r in range(N):
        for q in range(N):
            for f in range(F):
                v = pick(T[q], L[r, np.arange(8), q, f, o[r, :, q, f]]) + rng.integers(-10, 11, (8, 16, K))
                m = rng.random((8, 16, K)) < share[r, :, q, f][:, None, None]
                B[r, :, :, q, f] = np.clip(np.where(m, v, rng.integers(-V, V + 1, (8, 16, K))), -V, V)
    return B
def pack(R, B, L):
    return {"ref0": np.ascontiguousarray(R.reshape(N, 128, W)).astype(np.float32).astype(BF), "obs": np.ascontiguousarray(B.reshape(N, 128, N * F * K)).astype(np.float32).astype(BF),
            "ops": np.stack([gtable(a.reshape(8, -1)) for a in L])}
def setup_inputs(rng):
    T = rng.integers(-200, 201, (N, 8, 16, W)); R = T + rng.integers(-40, 41, T.shape); L = draw_lists(rng)
    share = rng.choice(np.array([1.0, 0.3, 0.02, 0.0]), (N, 8, N, F))
    return pack(R, frames(rng, T, L, share), L)
def setup_inputs_chain(rng):
    R = rng.integers(-200, 201, (N, 8, 16, W)); L = draw_lists(rng); B = np.zeros((N, 8, 16, N, F, K), np.int64)
    for q in range(N):
        for g in range(8):
            c = rng.permutation(W); P, Q = c[:K], c[K:2 * K]; R[q, g][:, Q] = R[q, g][:, P]
            away = rng.integers(1, 51, (16, K)) * (2 * rng.integers(0, 2, (16, K)) - 1)
            for r in range(N):
                for f in range(F):
                    z = rng.permutation(K); o = rng.permutation(O); e = 1 if rng.random() < 0.7 else -1
                    L[r, g, q, f, o[0]] = P[z]; L[r, g, q, f, o[1]] = Q[z]
                    B[r, g, :, q, f] = (R[q, g][:, P] + e * away)[:, z]
    return pack(R, B, L)
def setup_inputs_edges(rng):
    R = rng.integers(-200, 201, (N, 8, 16, W)); L = draw_lists(rng); B = np.zeros((N, 8, 16, N, F, K), np.int64)
    o = rng.integers(0, O, (N, 8, N, F)); same = rng.random((N, 8, N, F)) < 0.3
    for q in range(N):
        same[q, 0, q, 0] = True; same[q, 1, q, 0] = False
        for r in range(N):
            for f in range(F):
                s = rng.choice(np.array([0, 1, C - 1, C, C + 1, 2 * C]), (8, 16, K)) * (2 * rng.integers(0, 2, (8, 16, K)) - 1)
                B[r, :, :, q, f] = pick(R[q], L[r, np.arange(8), q, f, o[r, :, q, f]]) + np.where(same[r, :, q, f][:, None, None], 0, s)
    return pack(R, B, L)
def setup_inputs_ends(rng):
    R = rng.integers(10, V + 1, (N, 8, 16, W)); L = draw_lists(rng); B = rng.choice(np.array([-V, 1 - V, -1, 0, 1, V - 1, V]), (N, 8, 16, N, F, K))
    runs = [np.arange(K), np.arange(W - K, W), np.arange(K)[::-1], np.arange(W - 1, W - 1 - K, -1), np.arange(K) * (W // K)]
    z = rng.permuted(np.tile(np.arange(8), (N, 1)), axis=1)
    for q in range(N):
        for g in range(8):
            s = 2 * int(rng.integers(0, 2)) - 1; k = int(z[q, g])
            for r in range(N):
                for f in range(F):
                    for o in range(O):
                        i = int(rng.integers(0, len(runs) + 1))
                        L[r, g, q, f, o] = runs[i] if i < len(runs) else np.concatenate([[W - 1], 1 + rng.permutation(W - 2)[:K - 2], [0]])
            if k < 4: R[q, g] = rng.integers(V - 1 if k < 2 else 200, V + 1, (16, W))
            c = rng.permutation(W)
            for t in range(N * F if k % 2 == 1 else 1):
                r, f = (q + t // F) % N, t % F; p1, p2 = c[K - 1 + 2 * t], c[K + 2 * t]
                i = int(rng.integers(0, 16)); a = 259 + (k // 2) % 2 + 4 * int(rng.integers(0, 59)) - V
                R[q, g][:, p2] = R[q, g][:, p1]; R[q, g, i, p1] = a; R[q, g, i, p2] = a + 1
                near = np.append(c[:K - 1], p1); far = np.append(c[:K - 1], p2)
                w = int(rng.integers(1, O))
                if k == 0:
                    w = 1 + 3 * int(rng.integers(0, (O + 1) // 3))
                    if int(np.sum(R[q, g][:, near] + V)) % 2 == 1: R[q, g, 0, c[0]] = 2 * V - 1 - R[q, g, 0, c[0]]
                if k in (2, 3): w = 1 + 2 * int(rng.integers(0, O // 2))
                B[r, g, :, q, f] = -s * V
                for o in range(O): L[r, g, q, f, o] = rng.permutation(near if o == w else far)
            R[q, g] = s * R[q, g]
    return pack(R, B, L)
def setup_inputs_ties(rng):
    s = 2 * rng.integers(0, 2, (N, 8, 16, 1)) - 1; m = rng.integers(N * F * C - V, V - 2 * C, (N, 8, 16, 1))
    R = m + rng.integers(C, 2 * C + 1, (N, 8, 16, W)); R[..., W - 1] = V
    L = np.zeros((N, 8, N, F, O, K), np.int64); B = np.zeros((N, 8, 16, N, F, K), np.int64)
    for q in range(N):
        for g in range(8):
            S = rng.permutation(W - 1)[:K]
            for t in range(N * F):
                r, f = (q + t // F) % N, t % F
                if rng.random() < 0.5: S = rng.permutation(W - 1)[:K]
                w = int(rng.integers(0, O))
                for o in range(O):
                    p = rng.permutation(S)
                    if o < w or (o > w and rng.random() < 0.5): p[rng.integers(0, K)] = W - 1
                    L[r, g, q, f, o] = p
                B[r, g, :, q, f] = s[q, g] * (m[q, g] - t * C + rng.integers(0, C + 1, (16, K)))
    return pack(R * s, B, L)
def setup_inputs_spread(rng):
    z = np.exp2(-rng.integers(0, 9, (N, 8, 1, W)).astype(np.float64))
    T = (rng.integers(-V, V + 1, (N, 8, 16, W)) * z).astype(np.int64); R = np.clip(T + (rng.integers(-60, 61, T.shape) * z).astype(np.int64), -V, V); L = draw_lists(rng)
    share = rng.choice(np.array([1.0, 0.6, 0.1, 0.02, 0.0]), (N, 8, N, F))
    return pack(R, frames(rng, T, L, share), L)
def check_inputs(d):
    bad = []
    for k in ("ref0", "obs"):
        v = np.asarray(d[k]).astype(np.float32)
        if not (np.all(np.abs(v) <= V) and np.all(v == np.rint(v))): bad.append("range of " + k)
    if np.min(d["ops"]) < 0 or np.max(d["ops"]) > W - 1: bad.append("range of ops")
    for a in d["ops"]:
        e = np.sort(gentries(a).reshape(8, -1, K), axis=-1)
        if np.any(e[..., 1:] == e[..., :-1]):
            bad.append("repeated number in a list of ops"); break
    return bad
def reference(ref0, obs, ops):
    R = ref0.astype(np.float32).astype(np.int32).reshape(N, 8, 16, W); x = obs.astype(np.float32).astype(np.int32).reshape(N, 8, 16, N, F, K)
    L = np.stack([gentries(a) for a in ops]).astype(np.int64).reshape(N, 8, N, F, O, K)
    g, i = np.arange(8)[:, None, None], np.arange(16)[None, :, None]
    for q in range(N):
        for d in range(N):
            r = (q + d) % N
            for f in range(F):
                b = x[r, :, :, q, f]
                cost = np.stack([np.sum(np.abs(b - pick(R[q], L[r, :, q, f, o])), axis=(1, 2)) for o in range(O)])
                win = np.argmin(cost, axis=0)
                ix = L[r, np.arange(8), q, f, win]
                v = pick(R[q], ix)
                R[q][g, i, ix[:, None, :]] = v + np.clip(b - v, -C, C)
    return {"y": R.reshape(N, 128, W).astype(np.float32).astype(BF)}

@@ -1,0 +1,229 @@
+import numpy as np
+from concourse.mybir import dt, AluOpType, AxisListType, ActivationFunctionType
+
+N, W, K, F, O, C = 4, 4096, 640, 2, 4, 8
+LC = K // 16
+FC = O * LC
+H = K // 2
+
+SCRATCH = {
+    "ref": ("sbuf", [128, W], "bfloat16"),
+    "obsb": ("sbuf", [128, N * F * K], "bfloat16"),
+    "opsb": ("sbuf", [128, N * F * FC], "int32"),
+    "lo1": ("sbuf", [128, F * K], "bfloat16"),
+    "lo2": ("sbuf", [128, F * K], "bfloat16"),
+    "lo3": ("sbuf", [128, F * K], "bfloat16"),
+    "ll1": ("sbuf", [128, F * FC], "int32"),
+    "ll2": ("sbuf", [128, F * FC], "int32"),
+    "ll3": ("sbuf", [128, F * FC], "int32"),
+    "offs": ("sbuf", [128, N * F * FC], "uint16"),
+    "d0": ("sbuf", [128, K], "float32"),
+    "d1": ("sbuf", [128, K], "float32"),
+    "v2": ("sbuf", [128, K], "bfloat16"),
+    "v3": ("sbuf", [128, K], "bfloat16"),
+    "junk2": ("sbuf", [128, K], "float32"),
+    "junk3": ("sbuf", [128, K], "float32"),
+    "acc": ("sbuf", [128, 8], "float32"),
+    "pmin": ("sbuf", [128, 8], "float32"),
+    "flag": ("sbuf", [128, 8], "float32"),
+    "wcol": ("sbuf", [128, 8], "float32"),
+    "big": ("sbuf", [128, 8], "float32"),
+    "sel": ("sbuf", [128, 16], "uint16"),
+    "offw": ("sbuf", [128, 48], "uint16"),
+    "dh": ("sbuf", [128, H], "bfloat16"),
+    "dc": ("sbuf", [128, H], "bfloat16"),
+    "vw": ("sbuf", [128, K], "bfloat16"),
+    "ew": ("sbuf", [128, K], "bfloat16"),
+    "onesf": ("sbuf", [128, 128], "float32"),
+    "blk0": ("sbuf", [128, 128], "float32"),
+    "blk": ("sbuf", [128, 128], "float32"),
+    "onesb": ("sbuf", [128, 128], "bfloat16"),
+    "negb": ("sbuf", [128, 128], "bfloat16"),
+    "eye": ("sbuf", [128, 128], "bfloat16"),
+    "neye": ("sbuf", [128, 128], "bfloat16"),
+    "ip": ("sbuf", [128, 4], "int32"),
+    "ia": ("sbuf", [128, 4], "int32"),
+    "ic": ("sbuf", [128, 4], "int32"),
+    "bs": ("sbuf", [128, 4], "float32"),
+    "base": ("sbuf", [128, 4], "float32"),
+    "psa": ("psum", [128, 1024], "float32"),
+    "psb": ("psum", [128, 1024], "float32"),
+    "psc": ("psum", [128, 512], "float32"),
+    "psd": ("psum", [128, 512], "float32"),
+}
+SEMAPHORES = ["cv", "cs", "cp", "cg", "lops", "lobs0", "lobs1", "lref", "lsend1", "lsend2", "lsend3",
+              "arr1", "arr2", "arr3", "sent", "yst"]
+
+
+def rank_program(g, core, T, topo):
+    q = T.rank_of(core)
+    if q is None:
+        return
+    A, X, FN = AluOpType, AxisListType, ActivationFunctionType
+    queue = {"v": g.vector, "s": g.scalar, "p": g.tensor, "g": g}
+    count = {"cv": 0, "cs": 0, "cp": 0, "cg": 0}
+    seen = {"v": {}, "s": {}, "p": {}, "g": {}}
+
+    def need(e, deps):
+        top = {}
+        for name, n in deps:
+            top[name] = max(top.get(name, 0), n)
+        for name in top:
+            if seen[e].get(name, 0) < top[name]:
+                queue[e].wait_ge(T.sem[name], top[name])
+                seen[e][name] = top[name]
+
+    def done(e, inst):
+        name = "c" + e
+        inst.then_inc(T.sem[name], 1)
+        count[name] += 1
+        return (name, count[name])
+
+    g.sync.dma_start(T.ref[:], T.ref0[:]).then_inc(T.sem.lref, 16)
+    oc, bc = q * F * FC, q * F * K
+    g.scalar.dma_start(T.opsb[:, oc:oc + F * FC], T.ops[:, oc:oc + F * FC]).then_inc(T.sem.lops, 16)
+    g.scalar.dma_start(T.obsb[:, bc:bc + K], T.obs[:, bc:bc + K]).then_inc(T.sem.lobs0, 16)
+    g.scalar.dma_start(T.obsb[:, bc + K:bc + 2 * K], T.obs[:, bc + K:bc + 2 * K]).then_inc(T.sem.lobs1, 16)
+    for d in range(1, N):
+        o = (q - d) % N
+        s = T.sem["lsend%d" % d]
+        g.sync.dma_start(T.opsb[:, o * F * FC:(o + 1) * F * FC], T.ops[:, o * F * FC:(o + 1) * F * FC]).then_inc(s, 16)
+        g.sync.dma_start(T.obsb[:, o * F * K:(o + 1) * F * K], T.obs[:, o * F * K:(o + 1) * F * K]).then_inc(s, 16)
+
+    m1 = done("v", g.vector.memset(T.onesb[:], 1.0))
+    m2 = done("v", g.vector.memset(T.negb[:], -1.0))
+    m3 = done("v", g.vector.memset(T.onesf[:], 1.0))
+    mb = done("v", g.vector.memset(T.big[:], 1.0e9))
+    i1 = done("g", g.iota(T.ip[:], [[16, 4]], 0, 1))
+    i2 = done("g", g.iota(T.ic[:], [[16, 4]], 0, 0))
+    need("g", [m1])
+    te = done("g", g.affine_select(T.eye[:], T.onesb[:], [[-1, 128]], A.is_equal, 0.0, 0, 1))
+    need("g", [m2])
+    tn = done("g", g.affine_select(T.neye[:], T.negb[:], [[-1, 128]], A.is_equal, 0.0, 0, 1))
+    need("g", [m3])
+    b0 = done("g", g.affine_select(T.blk0[:], T.onesf[:], [[-16, 8], [0, 16]], A.is_ge, 0.0, 0, 1))
+    need("g", [b0])
+    tb = done("g", g.affine_select(T.blk[:], T.blk0[:], [[16, 8], [0, 16]], A.is_ge, 0.0, 15, -1))
+    need("v", [i1])
+    k1 = done("v", g.vector.tensor_scalar(T.ia[:], T.ip[:], 15, None, A.bitwise_and))
+    need("v", [k1, i2])
+    k2 = done("v", g.vector.tensor_tensor(T.bs[:], T.ia[:], T.ic[:], A.add))
+    need("v", [k2])
+    kbase = done("v", g.vector.tensor_scalar(T.base[:], T.bs[:], float(LC - 1), None, A.min))
+
+    nsent = 0
+    for d in range(1, N):
+        o = (q - d) % N
+        dst = T.cores[o]
+        rid, pid, _ = topo.addr(dst)
+        mask = topo.mask(core, dst)
+        ne = len(topo.engines(core, dst))
+        g.wait_ge(T.sem["lsend%d" % d], 32)
+        for land, src in ((T["ll%d" % d], T.opsb[:, o * F * FC:(o + 1) * F * FC]),
+                          (T["lo%d" % d], T.obsb[:, o * F * K:(o + 1) * F * K])):
+            g.remote_dma(land[:], src, T.sem["arr%d" % d], T.sem.sent, pid, rid, mask)
+            nsent += ne
+
+    def frame(t):
+        d, f = t // F, t % F
+        if d == 0:
+            b = T.obsb
+            c0 = bc + f * K
+            dep = [("lobs%d" % f, 16)]
+            ldep = [("lops", 16)]
+            lw = T.opsb[:, oc + f * FC:oc + (f + 1) * FC]
+        else:
+            b = T["lo%d" % d]
+            c0 = f * K
+            src = T.cores[(q + d) % N]
+            dep = ldep = [("arr%d" % d, 2 * len(topo.engines(src, core)))]
+            lw = T["ll%d" % d][:, f * FC:(f + 1) * FC]
+        return b, c0, dep, lw, ldep
+
+    def convert(t):
+        _, _, _, lw, ldep = frame(t)
+        need("v", ldep)
+        return done("v", g.vector.tensor_copy(T.offs[:, t * FC:(t + 1) * FC], lw))
+
+    def mm(out, lhsT, rhs, start, stop):
+        return done("p", g.tensor.matmul(out, lhsT, rhs, start, stop))
+
+    def way_mm(ps, lhsT, rhs_t, c0, start):
+        mm(ps[:, 0:512], lhsT[:], rhs_t[:, c0:c0 + 512], start, not start)
+        return mm(ps[:, 512:K], lhsT[:], rhs_t[:, c0 + 512:c0 + K], start, not start)
+
+    def lay(t, free_a, free_b, free_d):
+        b, c0, dep, _, _ = frame(t)
+        need("p", dep + free_a)
+        way_mm(T.psa, T.neye, b, c0, True)
+        need("p", free_b)
+        way_mm(T.psb, T.neye, b, c0, True)
+        need("p", free_d)
+        mm(T.psd[:, 0:H], T.eye[:], b[:, c0 + H:c0 + K], True, False)
+
+    conv = {0: convert(0), 1: convert(1)}
+    need("p", [te, tn, tb])
+    lay(0, [], [], [])
+
+    ready = [("lref", 16)]
+    win = T.ref[:, 0:W]
+    NT = N * F
+    for t in range(NT):
+        b, c0, dep, lw, _ = frame(t)
+        off = lambda a: T.offs[:, t * FC + a * LC:t * FC + (a + 1) * LC]
+        need("v", ready + dep + [conv[t]])
+        g0 = done("v", g.vector.tensor_tensor(T.d0[:], win.indirect(off(0)), b[:, c0:c0 + K], A.subtract))
+        g1 = done("v", g.vector.tensor_tensor(T.d1[:], win.indirect(off(1)), b[:, c0:c0 + K], A.subtract))
+        need("s", ready + [conv[t]])
+        g2 = done("s", g.scalar.activation(T.v2[:], win.indirect(off(2)), FN.Identity))
+        g3 = done("s", g.scalar.activation(T.v3[:], win.indirect(off(3)), FN.Identity))
+        need("p", [g2])
+        w2 = way_mm(T.psa, T.eye, T.v2, 0, False)
+        need("p", [g3])
+        w3 = way_mm(T.psb, T.eye, T.v3, 0, False)
+        need("v", [g0])
+        done("v", g.vector.tensor_reduce(T.acc[:, 0:1], T.d0[:], X.X, A.add, apply_absolute_value=True))
+        need("v", [g1])
+        r1 = done("v", g.vector.tensor_reduce(T.acc[:, 1:2], T.d1[:], X.X, A.add, apply_absolute_value=True))
+        need("s", [w2])
+        a2 = done("s", g.scalar.activation(T.junk2[:], T.psa[:, 0:K], FN.Abs, accum_out=T.acc[:, 2:3]))
+        need("s", [w3])
+        a3 = done("s", g.scalar.activation(T.junk3[:], T.psb[:, 0:K], FN.Abs, accum_out=T.acc[:, 3:4]))
+        need("p", [r1, a3])
+        el = mm(T.psc[:, 0:O], T.blk[:], T.acc[:, 0:O], True, True)
+        if 1 <= t < NT - 1:
+            conv[t + 1] = convert(t + 1)
+        need("v", [el, mb])
+        e1 = done("v", g.vector.tensor_tensor_scan(T.pmin[:, 0:O], T.psc[:, 0:O], T.big[:, 0:O], 1.0e9, A.min, A.min))
+        need("v", [e1])
+        e2 = done("v", g.vector.tensor_scalar(T.flag[:, 0:O - 1], T.pmin[:, 0:O - 1], T.pmin[:, O - 1:O], float(LC), A.is_gt, A.mult))
+        need("v", [e2])
+        e3 = done("v", g.vector.tensor_reduce(T.wcol[:, 0:1], T.flag[:, 0:O - 1], X.X, A.add))
+        need("v", [e3, kbase])
+        e4 = done("v", g.vector.tensor_scalar(T.sel[:, 0:3], T.base[:, 0:3], T.wcol[:, 0:1], None, A.add))
+        need("v", [e4])
+        e5 = done("v", g.vector.tensor_copy(T.offw[:, 0:48], lw.indirect(T.sel[:, 0:3])))
+        need("v", [e5])
+        x1 = done("v", g.vector.tensor_tensor(T.dh[:], win.indirect(T.offw[:, 0:LC // 2]), b[:, c0:c0 + H], A.subtract))
+        need("s", [e5])
+        s2 = done("s", g.scalar.activation(T.vw[:, H:K], win.indirect(T.offw[:, LC // 2:LC]), FN.Identity))
+        s1 = done("s", g.scalar.activation(T.vw[:, 0:H], win.indirect(T.offw[:, 0:LC // 2]), FN.Identity))
+        need("p", [s2])
+        x2 = mm(T.psd[:, 0:H], T.neye[:], T.vw[:, H:K], False, True)
+        need("v", [x1])
+        x3 = done("v", g.vector.tensor_scalar(T.dc[:], T.dh[:], -1.0, float(C), A.mult, A.min))
+        need("v", [x3])
+        x4 = done("v", g.vector.tensor_scalar(T.ew[:, 0:H], T.dc[:], float(-C), None, A.max))
+        need("v", [x2])
+        x5 = done("v", g.vector.tensor_scalar(T.ew[:, H:K], T.psd[:, 0:H], float(C), float(-C), A.min, A.max))
+        need("v", [x4, x5, s1])
+        sc = done("v", g.vector.tensor_tensor(win.indirect(T.offw[:, 0:LC]), T.vw[:], T.ew[:], A.add))
+        ready = [sc]
+        if t < NT - 1:
+            lay(t + 1, [a2], [a3], [x5])
+
+    g.sync.wait_ge(T.sem.cv, count["cv"])
+    g.sync.dma_start(T.y[:], T.ref[:]).then_inc(T.sem.yst, 16)
+    g.sync.wait_ge(T.sem.yst, 16)
+    g.wait_ge(T.sem.sent, nsent)
+    need("g", [(c, count[c]) for c in ("cv", "cs", "cp", "cg")])

@@ -4,7 +4,10 @@ from concourse.mybir import dt, AluOpType, AxisListType, ActivationFunctionType
 N, W, K, F, O, C = 4, 4096, 640, 2, 4, 8
 LC = K // 16
 FC = O * LC
-H = K // 2
+Y = 64
+KY = K - Y
+VB, HC, A1 = 2, 18, 12
+B1, H1, HA = 16 * VB, 16 * HC, 16 * (HC + A1)
 
 SCRATCH = {
     "ref": ("sbuf", [128, W], "bfloat16"),
@@ -22,16 +25,17 @@ SCRATCH = {
     "v2": ("sbuf", [128, K], "bfloat16"),
     "v3": ("sbuf", [128, K], "bfloat16"),
     "junk2": ("sbuf", [128, K], "float32"),
-    "junk3": ("sbuf", [128, K], "float32"),
+    "junk3": ("sbuf", [128, KY], "float32"),
     "acc": ("sbuf", [128, 8], "float32"),
-    "pmin": ("sbuf", [128, 8], "float32"),
+    "accb": ("sbuf", [128, 8], "float32"),
+    "nmax": ("sbuf", [128, 8], "float32"),
     "flag": ("sbuf", [128, 8], "float32"),
     "wcol": ("sbuf", [128, 8], "float32"),
-    "big": ("sbuf", [128, 8], "float32"),
+    "low": ("sbuf", [128, 8], "float32"),
     "sel": ("sbuf", [128, 16], "uint16"),
     "offw": ("sbuf", [128, 48], "uint16"),
-    "dh": ("sbuf", [128, H], "bfloat16"),
-    "dc": ("sbuf", [128, H], "bfloat16"),
+    "dh": ("sbuf", [128, H1], "bfloat16"),
+    "dc": ("sbuf", [128, H1], "bfloat16"),
     "vw": ("sbuf", [128, K], "bfloat16"),
     "ew": ("sbuf", [128, K], "bfloat16"),
     "onesf": ("sbuf", [128, 128], "float32"),
@@ -45,13 +49,16 @@ SCRATCH = {
     "ia": ("sbuf", [128, 4], "int32"),
     "ic": ("sbuf", [128, 4], "int32"),
     "bs": ("sbuf", [128, 4], "float32"),
+    "bt": ("sbuf", [128, 4], "float32"),
     "base": ("sbuf", [128, 4], "float32"),
     "psa": ("psum", [128, 1024], "float32"),
     "psb": ("psum", [128, 1024], "float32"),
     "psc": ("psum", [128, 512], "float32"),
     "psd": ("psum", [128, 512], "float32"),
+    "psf": ("psum", [128, 512], "float32"),
+    "psg": ("psum", [128, 512], "float32"),
 }
-SEMAPHORES = ["cv", "cs", "cp", "cg", "lops", "lobs0", "lobs1", "lref", "lsend1", "lsend2", "lsend3",
+SEMAPHORES = ["cv", "cs", "cp", "cg", "lops0", "lops1", "lobs0", "lobs1", "lref", "lsend1", "lsend2", "lsend3",
               "arr1", "arr2", "arr3", "sent", "yst"]
 
 
@@ -79,11 +86,12 @@ def rank_program(g, core, T, topo):
         count[name] += 1
         return (name, count[name])
 
-    g.sync.dma_start(T.ref[:], T.ref0[:]).then_inc(T.sem.lref, 16)
     oc, bc = q * F * FC, q * F * K
-    g.scalar.dma_start(T.opsb[:, oc:oc + F * FC], T.ops[:, oc:oc + F * FC]).then_inc(T.sem.lops, 16)
+    g.sync.dma_start(T.opsb[:, oc:oc + FC], T.ops[:, oc:oc + FC]).then_inc(T.sem.lops0, 16)
     g.scalar.dma_start(T.obsb[:, bc:bc + K], T.obs[:, bc:bc + K]).then_inc(T.sem.lobs0, 16)
-    g.scalar.dma_start(T.obsb[:, bc + K:bc + 2 * K], T.obs[:, bc + K:bc + 2 * K]).then_inc(T.sem.lobs1, 16)
+    g.sync.dma_start(T.ref[:], T.ref0[:]).then_inc(T.sem.lref, 16)
+    g.sync.dma_start(T.opsb[:, oc + FC:oc + 2 * FC], T.ops[:, oc + FC:oc + 2 * FC]).then_inc(T.sem.lops1, 16)
+    g.sync.dma_start(T.obsb[:, bc + K:bc + 2 * K], T.obs[:, bc + K:bc + 2 * K]).then_inc(T.sem.lobs1, 16)
     for d in range(1, N):
         o = (q - d) % N
         s = T.sem["lsend%d" % d]
@@ -92,8 +100,9 @@ def rank_program(g, core, T, topo):
 
     m1 = done("v", g.vector.memset(T.onesb[:], 1.0))
     m2 = done("v", g.vector.memset(T.negb[:], -1.0))
-    m3 = done("v", g.vector.memset(T.onesf[:], 1.0))
-    mb = done("v", g.vector.memset(T.big[:], 1.0e9))
+    m3 = done("v", g.vector.memset(T.onesf[:], -1.0))
+    done("v", g.vector.memset(T.low[:], -1.0e9))
+    mz = done("v", g.vector.memset(T.accb[:], 0.0))
     i1 = done("g", g.iota(T.ip[:], [[16, 4]], 0, 1))
     i2 = done("g", g.iota(T.ic[:], [[16, 4]], 0, 0))
     need("g", [m1])
@@ -109,7 +118,9 @@ def rank_program(g, core, T, topo):
     need("v", [k1, i2])
     k2 = done("v", g.vector.tensor_tensor(T.bs[:], T.ia[:], T.ic[:], A.add))
     need("v", [k2])
-    kbase = done("v", g.vector.tensor_scalar(T.base[:], T.bs[:], float(LC - 1), None, A.min))
+    k3 = done("v", g.vector.tensor_scalar(T.bt[:], T.bs[:], float(LC - 1), 0.25, A.min, A.add))
+    need("v", [k3])
+    kbase = done("v", g.vector.tensor_scalar(T.base[:], T.bt[:], 1.0 / LC, None, A.mult))
 
     nsent = 0
     for d in range(1, N):
@@ -130,7 +141,7 @@ def rank_program(g, core, T, topo):
             b = T.obsb
             c0 = bc + f * K
             dep = [("lobs%d" % f, 16)]
-            ldep = [("lops", 16)]
+            ldep = [("lops%d" % f, 16)]
             lw = T.opsb[:, oc + f * FC:oc + (f + 1) * FC]
         else:
             b = T["lo%d" % d]
@@ -148,29 +159,33 @@ def rank_program(g, core, T, topo):
     def mm(out, lhsT, rhs, start, stop):
         return done("p", g.tensor.matmul(out, lhsT, rhs, start, stop))
 
-    def way_mm(ps, lhsT, rhs_t, c0, start):
+    def way_mm(ps, lhsT, rhs_t, c0, n, start):
         mm(ps[:, 0:512], lhsT[:], rhs_t[:, c0:c0 + 512], start, not start)
-        return mm(ps[:, 512:K], lhsT[:], rhs_t[:, c0 + 512:c0 + K], start, not start)
+        return mm(ps[:, 512:n], lhsT[:], rhs_t[:, c0 + 512:c0 + n], start, not start)
 
     def lay(t, free_a, free_b, free_d):
         b, c0, dep, _, _ = frame(t)
         need("p", dep + free_a)
-        way_mm(T.psa, T.neye, b, c0, True)
+        way_mm(T.psa, T.neye, b, c0, K, True)
         need("p", free_b)
-        way_mm(T.psb, T.neye, b, c0, True)
+        mm(T.psg[:, 0:Y], T.neye[:], b[:, c0 + KY:c0 + K], True, False)
+        way_mm(T.psb, T.neye, b, c0, KY, True)
         need("p", free_d)
-        mm(T.psd[:, 0:H], T.eye[:], b[:, c0 + H:c0 + K], True, False)
+        mm(T.psd[:, 0:HA - H1], T.eye[:], b[:, c0 + H1:c0 + HA], True, False)
+        mm(T.psf[:, 0:K - HA], T.eye[:], b[:, c0 + HA:c0 + K], True, False)
 
-    conv = {0: convert(0), 1: convert(1)}
-    need("p", [te, tn, tb])
+    conv = {0: convert(0)}
+    need("p", [te, tn])
     lay(0, [], [], [])
+    need("p", [tb, mz])
 
     ready = [("lref", 16)]
     win = T.ref[:, 0:W]
     NT = N * F
     for t in range(NT):
         b, c0, dep, lw, _ = frame(t)
-        off = lambda a: T.offs[:, t * FC + a * LC:t * FC + (a + 1) * LC]
+        lo = t * FC
+        off = lambda a: T.offs[:, lo + a * LC:lo + (a + 1) * LC]
         need("v", ready + dep + [conv[t]])
         g0 = done("v", g.vector.tensor_tensor(T.d0[:], win.indirect(off(0)), b[:, c0:c0 + K], A.subtract))
         g1 = done("v", g.vector.tensor_tensor(T.d1[:], win.indirect(off(1)), b[:, c0:c0 + K], A.subtract))
@@ -178,49 +193,59 @@ def rank_program(g, core, T, topo):
         g2 = done("s", g.scalar.activation(T.v2[:], win.indirect(off(2)), FN.Identity))
         g3 = done("s", g.scalar.activation(T.v3[:], win.indirect(off(3)), FN.Identity))
         need("p", [g2])
-        w2 = way_mm(T.psa, T.eye, T.v2, 0, False)
+        w2 = way_mm(T.psa, T.eye, T.v2, 0, K, False)
         need("p", [g3])
-        w3 = way_mm(T.psb, T.eye, T.v3, 0, False)
+        wy = mm(T.psg[:, 0:Y], T.eye[:], T.v3[:, KY:K], False, True)
+        w3 = way_mm(T.psb, T.eye, T.v3, 0, KY, False)
         need("v", [g0])
         done("v", g.vector.tensor_reduce(T.acc[:, 0:1], T.d0[:], X.X, A.add, apply_absolute_value=True))
+        need("v", [wy])
+        ry = done("v", g.vector.tensor_reduce(T.accb[:, 3:4], T.psg[:, 0:Y], X.X, A.add, apply_absolute_value=True))
         need("v", [g1])
         r1 = done("v", g.vector.tensor_reduce(T.acc[:, 1:2], T.d1[:], X.X, A.add, apply_absolute_value=True))
         need("s", [w2])
         a2 = done("s", g.scalar.activation(T.junk2[:], T.psa[:, 0:K], FN.Abs, accum_out=T.acc[:, 2:3]))
         need("s", [w3])
-        a3 = done("s", g.scalar.activation(T.junk3[:], T.psb[:, 0:K], FN.Abs, accum_out=T.acc[:, 3:4]))
+        a3 = done("s", g.scalar.activation(T.junk3[:], T.psb[:, 0:KY], FN.Abs, accum_out=T.acc[:, 3:4]))
+        need("p", [ry])
+        mm(T.psc[:, 0:O], T.blk[:], T.accb[:, 0:O], True, False)
         need("p", [r1, a3])
-        el = mm(T.psc[:, 0:O], T.blk[:], T.acc[:, 0:O], True, True)
-        if 1 <= t < NT - 1:
+        el = mm(T.psc[:, 0:O], T.blk[:], T.acc[:, 0:O], False, True)
+        if t < NT - 1:
             conv[t + 1] = convert(t + 1)
-        need("v", [el, mb])
-        e1 = done("v", g.vector.tensor_tensor_scan(T.pmin[:, 0:O], T.psc[:, 0:O], T.big[:, 0:O], 1.0e9, A.min, A.min))
-        need("v", [e1])
-        e2 = done("v", g.vector.tensor_scalar(T.flag[:, 0:O - 1], T.pmin[:, 0:O - 1], T.pmin[:, O - 1:O], float(LC), A.is_gt, A.mult))
-        need("v", [e2])
-        e3 = done("v", g.vector.tensor_reduce(T.wcol[:, 0:1], T.flag[:, 0:O - 1], X.X, A.add))
+        need("v", [el])
+        e1 = done("v", g.vector.tensor_tensor_scan(T.nmax[:, 0:O], T.psc[:, 0:O], T.low[:, 0:O], -1.0e9, A.max, A.max))
+        need("s", [e1])
+        e3 = done("s", g.scalar.activation(T.flag[:, 0:O - 1], T.nmax[:, 0:O - 1], FN.Sign, bias=T.nmax[:, O - 1:O], scale=-1.0,
+                                           accum_out=T.wcol[:, 0:1]))
         need("v", [e3, kbase])
-        e4 = done("v", g.vector.tensor_scalar(T.sel[:, 0:3], T.base[:, 0:3], T.wcol[:, 0:1], None, A.add))
+        e4 = done("v", g.vector.tensor_scalar(T.sel[:, 0:3], T.base[:, 0:3], T.wcol[:, 0:1], float(LC), A.add, A.mult))
         need("v", [e4])
         e5 = done("v", g.vector.tensor_copy(T.offw[:, 0:48], lw.indirect(T.sel[:, 0:3])))
         need("v", [e5])
-        x1 = done("v", g.vector.tensor_tensor(T.dh[:], win.indirect(T.offw[:, 0:LC // 2]), b[:, c0:c0 + H], A.subtract))
+        x1 = done("v", g.vector.tensor_tensor(T.dh[:], win.indirect(T.offw[:, 0:HC]), b[:, c0:c0 + H1], A.subtract))
+        done("v", g.vector.tensor_copy(T.vw[:, 0:B1], win.indirect(T.offw[:, 0:VB])))
         need("s", [e5])
-        s2 = done("s", g.scalar.activation(T.vw[:, H:K], win.indirect(T.offw[:, LC // 2:LC]), FN.Identity))
-        s1 = done("s", g.scalar.activation(T.vw[:, 0:H], win.indirect(T.offw[:, 0:LC // 2]), FN.Identity))
+        s2 = done("s", g.scalar.activation(T.vw[:, H1:HA], win.indirect(T.offw[:, HC:HC + A1]), FN.Identity))
+        s3 = done("s", g.scalar.activation(T.vw[:, HA:K], win.indirect(T.offw[:, HC + A1:LC]), FN.Identity))
+        s1 = done("s", g.scalar.activation(T.vw[:, B1:H1], win.indirect(T.offw[:, VB:HC]), FN.Identity))
         need("p", [s2])
-        x2 = mm(T.psd[:, 0:H], T.neye[:], T.vw[:, H:K], False, True)
+        x2 = mm(T.psd[:, 0:HA - H1], T.neye[:], T.vw[:, H1:HA], False, True)
+        need("p", [s3])
+        x2b = mm(T.psf[:, 0:K - HA], T.neye[:], T.vw[:, HA:K], False, True)
         need("v", [x1])
         x3 = done("v", g.vector.tensor_scalar(T.dc[:], T.dh[:], -1.0, float(C), A.mult, A.min))
-        need("v", [x3])
-        x4 = done("v", g.vector.tensor_scalar(T.ew[:, 0:H], T.dc[:], float(-C), None, A.max))
         need("v", [x2])
-        x5 = done("v", g.vector.tensor_scalar(T.ew[:, H:K], T.psd[:, 0:H], float(C), float(-C), A.min, A.max))
+        done("v", g.vector.tensor_scalar(T.ew[:, H1:HA], T.psd[:, 0:HA - H1], float(C), float(-C), A.min, A.max))
+        need("v", [x3])
+        x4 = done("v", g.vector.tensor_scalar(T.ew[:, 0:H1], T.dc[:], float(-C), None, A.max))
+        need("v", [x2b])
+        x5 = done("v", g.vector.tensor_scalar(T.ew[:, HA:K], T.psf[:, 0:K - HA], float(C), float(-C), A.min, A.max))
         need("v", [x4, x5, s1])
         sc = done("v", g.vector.tensor_tensor(win.indirect(T.offw[:, 0:LC]), T.vw[:], T.ew[:], A.add))
         ready = [sc]
         if t < NT - 1:
-            lay(t + 1, [a2], [a3], [x5])
+            lay(t + 1, [a2], [a3, ry], [x5])
 
     g.sync.wait_ge(T.sem.cv, count["cv"])
     g.sync.dma_start(T.y[:], T.ref[:]).then_inc(T.sem.yst, 16)

@@ -4,10 +4,12 @@ from concourse.mybir import dt, AluOpType, AxisListType, ActivationFunctionType
 N, W, K, F, O, C = 4, 4096, 640, 2, 4, 8
 LC = K // 16
 FC = O * LC
-Y = 64
+Y = 104
 KY = K - Y
-VB, HC, A1 = 2, 18, 12
-B1, H1, HA = 16 * VB, 16 * HC, 16 * (HC + A1)
+HC, A1 = 20, 12
+H1, HA = 16 * HC, 16 * (HC + A1)
+R = K - 512
+E = 128
 
 SCRATCH = {
     "ref": ("sbuf", [128, W], "bfloat16"),
@@ -20,10 +22,9 @@ SCRATCH = {
     "ll2": ("sbuf", [128, F * FC], "int32"),
     "ll3": ("sbuf", [128, F * FC], "int32"),
     "offs": ("sbuf", [128, N * F * FC], "uint16"),
-    "d0": ("sbuf", [128, K], "float32"),
-    "d1": ("sbuf", [128, K], "float32"),
-    "v2": ("sbuf", [128, K], "bfloat16"),
-    "v3": ("sbuf", [128, K], "bfloat16"),
+    "d0": ("sbuf", [128, K], "float16"),
+    "d1": ("sbuf", [128, K], "float16"),
+    "vall": ("sbuf", [128, O * K], "bfloat16"),
     "junk2": ("sbuf", [128, K], "float32"),
     "junk3": ("sbuf", [128, KY], "float32"),
     "acc": ("sbuf", [128, 8], "float32"),
@@ -33,9 +34,9 @@ SCRATCH = {
     "wcol": ("sbuf", [128, 8], "float32"),
     "low": ("sbuf", [128, 8], "float32"),
     "sel": ("sbuf", [128, 16], "uint16"),
+    "selv": ("sbuf", [128, 48], "uint16"),
     "offw": ("sbuf", [128, 48], "uint16"),
-    "dh": ("sbuf", [128, H1], "bfloat16"),
-    "dc": ("sbuf", [128, H1], "bfloat16"),
+    "dw": ("sbuf", [128, H1], "bfloat16"),
     "vw": ("sbuf", [128, K], "bfloat16"),
     "ew": ("sbuf", [128, K], "bfloat16"),
     "onesf": ("sbuf", [128, 128], "float32"),
@@ -45,12 +46,14 @@ SCRATCH = {
     "negb": ("sbuf", [128, 128], "bfloat16"),
     "eye": ("sbuf", [128, 128], "bfloat16"),
     "neye": ("sbuf", [128, 128], "bfloat16"),
-    "ip": ("sbuf", [128, 4], "int32"),
-    "ia": ("sbuf", [128, 4], "int32"),
-    "ic": ("sbuf", [128, 4], "int32"),
-    "bs": ("sbuf", [128, 4], "float32"),
+    "neyeh": ("sbuf", [128, 128], "float16"),
+    "ip": ("sbuf", [128, LC], "int32"),
+    "ia": ("sbuf", [128, LC], "int32"),
+    "ic": ("sbuf", [128, LC], "int32"),
+    "bs": ("sbuf", [128, LC], "float32"),
     "bt": ("sbuf", [128, 4], "float32"),
     "base": ("sbuf", [128, 4], "float32"),
+    "basev": ("sbuf", [128, LC], "float32"),
     "psa": ("psum", [128, 1024], "float32"),
     "psb": ("psum", [128, 1024], "float32"),
     "psc": ("psum", [128, 512], "float32"),
@@ -59,7 +62,7 @@ SCRATCH = {
     "psg": ("psum", [128, 512], "float32"),
 }
 SEMAPHORES = ["cv", "cs", "cp", "cg", "lops0", "lops1", "lobs0", "lobs1", "lref", "lsend1", "lsend2", "lsend3",
-              "arr1", "arr2", "arr3", "sent", "yst"]
+              "llist1", "llist2", "llist3", "arr1", "arr2", "arr3", "sent", "yst"]
 
 
 def rank_program(g, core, T, topo):
@@ -90,21 +93,27 @@ def rank_program(g, core, T, topo):
     g.sync.dma_start(T.opsb[:, oc:oc + FC], T.ops[:, oc:oc + FC]).then_inc(T.sem.lops0, 16)
     g.scalar.dma_start(T.obsb[:, bc:bc + K], T.obs[:, bc:bc + K]).then_inc(T.sem.lobs0, 16)
     g.sync.dma_start(T.ref[:], T.ref0[:]).then_inc(T.sem.lref, 16)
+
+    def load(d):
+        o = (q - d) % N
+        g.sync.dma_start(T.opsb[:, o * F * FC:(o + 1) * F * FC],
+                         T.ops[:, o * F * FC:(o + 1) * F * FC]).then_inc(T.sem["llist%d" % d], 16)
+        g.sync.dma_start(T.obsb[:, o * F * K:(o + 1) * F * K],
+                         T.obs[:, o * F * K:(o + 1) * F * K]).then_inc(T.sem["lsend%d" % d], 16)
+
+    load(1)
     g.sync.dma_start(T.opsb[:, oc + FC:oc + 2 * FC], T.ops[:, oc + FC:oc + 2 * FC]).then_inc(T.sem.lops1, 16)
     g.sync.dma_start(T.obsb[:, bc + K:bc + 2 * K], T.obs[:, bc + K:bc + 2 * K]).then_inc(T.sem.lobs1, 16)
-    for d in range(1, N):
-        o = (q - d) % N
-        s = T.sem["lsend%d" % d]
-        g.sync.dma_start(T.opsb[:, o * F * FC:(o + 1) * F * FC], T.ops[:, o * F * FC:(o + 1) * F * FC]).then_inc(s, 16)
-        g.sync.dma_start(T.obsb[:, o * F * K:(o + 1) * F * K], T.obs[:, o * F * K:(o + 1) * F * K]).then_inc(s, 16)
+    load(2)
+    load(3)
 
     m1 = done("v", g.vector.memset(T.onesb[:], 1.0))
     m2 = done("v", g.vector.memset(T.negb[:], -1.0))
     m3 = done("v", g.vector.memset(T.onesf[:], -1.0))
     done("v", g.vector.memset(T.low[:], -1.0e9))
     mz = done("v", g.vector.memset(T.accb[:], 0.0))
-    i1 = done("g", g.iota(T.ip[:], [[16, 4]], 0, 1))
-    i2 = done("g", g.iota(T.ic[:], [[16, 4]], 0, 0))
+    i1 = done("g", g.iota(T.ip[:], [[16, LC]], 0, 1))
+    i2 = done("g", g.iota(T.ic[:], [[16, LC]], 0, 0))
     need("g", [m1])
     te = done("g", g.affine_select(T.eye[:], T.onesb[:], [[-1, 128]], A.is_equal, 0.0, 0, 1))
     need("g", [m2])
@@ -118,9 +127,12 @@ def rank_program(g, core, T, topo):
     need("v", [k1, i2])
     k2 = done("v", g.vector.tensor_tensor(T.bs[:], T.ia[:], T.ic[:], A.add))
     need("v", [k2])
-    k3 = done("v", g.vector.tensor_scalar(T.bt[:], T.bs[:], float(LC - 1), 0.25, A.min, A.add))
+    k3 = done("v", g.vector.tensor_scalar(T.bt[:], T.bs[:, 0:4], float(LC - 1), 0.25, A.min, A.add))
+    kbv = done("v", g.vector.tensor_scalar(T.basev[:], T.bs[:], 0.25, 1.0 / K, A.add, A.mult))
     need("v", [k3])
     kbase = done("v", g.vector.tensor_scalar(T.base[:], T.bt[:], 1.0 / LC, None, A.mult))
+    need("v", [tn])
+    th = done("v", g.vector.tensor_copy(T.neyeh[:], T.neye[:]))
 
     nsent = 0
     for d in range(1, N):
@@ -129,9 +141,9 @@ def rank_program(g, core, T, topo):
         rid, pid, _ = topo.addr(dst)
         mask = topo.mask(core, dst)
         ne = len(topo.engines(core, dst))
-        g.wait_ge(T.sem["lsend%d" % d], 32)
-        for land, src in ((T["ll%d" % d], T.opsb[:, o * F * FC:(o + 1) * F * FC]),
-                          (T["lo%d" % d], T.obsb[:, o * F * K:(o + 1) * F * K])):
+        for land, src, sem in ((T["ll%d" % d], T.opsb[:, o * F * FC:(o + 1) * F * FC], T.sem["llist%d" % d]),
+                               (T["lo%d" % d], T.obsb[:, o * F * K:(o + 1) * F * K], T.sem["lsend%d" % d])):
+            g.wait_ge(sem, 16)
             g.remote_dma(land[:], src, T.sem["arr%d" % d], T.sem.sent, pid, rid, mask)
             nsent += ne
 
@@ -157,95 +169,118 @@ def rank_program(g, core, T, topo):
         return done("v", g.vector.tensor_copy(T.offs[:, t * FC:(t + 1) * FC], lw))
 
     def mm(out, lhsT, rhs, start, stop):
-        return done("p", g.tensor.matmul(out, lhsT, rhs, start, stop))
+        return done("p", g.tensor.matmul(out, lhsT[:], rhs, start, stop))
 
-    def way_mm(ps, lhsT, rhs_t, c0, n, start):
-        mm(ps[:, 0:512], lhsT[:], rhs_t[:, c0:c0 + 512], start, not start)
-        return mm(ps[:, 512:n], lhsT[:], rhs_t[:, c0 + 512:c0 + n], start, not start)
+    psy = T.psc[:, 128:128 + Y]
 
-    def lay(t, free_a, free_b, free_d):
+    def lay(t, free_a, free_b, free_d, free_f):
         b, c0, dep, _, _ = frame(t)
         need("p", dep + free_a)
-        way_mm(T.psa, T.neye, b, c0, K, True)
-        need("p", free_b)
-        mm(T.psg[:, 0:Y], T.neye[:], b[:, c0 + KY:c0 + K], True, False)
-        way_mm(T.psb, T.neye, b, c0, KY, True)
+        mm(T.psa[:, 0:512], T.eye, b[:, c0:c0 + 512], True, False)
+        mm(T.psa[:, 512:K], T.eye, b[:, c0 + 512:c0 + K], True, False)
         need("p", free_d)
-        mm(T.psd[:, 0:HA - H1], T.eye[:], b[:, c0 + H1:c0 + HA], True, False)
-        mm(T.psf[:, 0:K - HA], T.eye[:], b[:, c0 + HA:c0 + K], True, False)
+        mm(T.psd[:, 0:512], T.neye, b[:, c0:c0 + 512], True, False)
+        need("p", free_b)
+        mm(T.psb[:, 0:512], T.eye, b[:, c0:c0 + 512], True, False)
+        mm(T.psb[:, 512:KY], T.eye, b[:, c0 + 512:c0 + KY], True, False)
+        mm(psy, T.eye, b[:, c0 + KY:c0 + K], True, False)
+        need("p", free_f)
+        mm(T.psf[:, 0:512], T.neye, b[:, c0:c0 + 512], True, False)
+
+    def values(o, ps, d, b, c0):
+        mm(ps[:, 0:512], T.neyeh, d[:, 0:512], False, True)
+        rest = T.psg[:, o * R:(o + 1) * R]
+        mm(rest, T.neye, b[:, c0 + 512:c0 + K], True, False)
+        return mm(rest, T.neyeh, d[:, 512:K], False, True)
 
     conv = {0: convert(0)}
     need("p", [te, tn])
-    lay(0, [], [], [])
-    need("p", [tb, mz])
+    lay(0, [], [], [], [])
+    need("p", [tb, mz, th])
 
     ready = [("lref", 16)]
     win = T.ref[:, 0:W]
+    vwin = T.vall[:, 0:O * K]
     NT = N * F
     for t in range(NT):
         b, c0, dep, lw, _ = frame(t)
-        lo = t * FC
-        off = lambda a: T.offs[:, lo + a * LC:lo + (a + 1) * LC]
+        off = lambda a: T.offs[:, t * FC + a * LC:t * FC + (a + 1) * LC]
+        val = lambda a: T.vall[:, a * K:(a + 1) * K]
         need("v", ready + dep + [conv[t]])
         g0 = done("v", g.vector.tensor_tensor(T.d0[:], win.indirect(off(0)), b[:, c0:c0 + K], A.subtract))
         g1 = done("v", g.vector.tensor_tensor(T.d1[:], win.indirect(off(1)), b[:, c0:c0 + K], A.subtract))
         need("s", ready + [conv[t]])
-        g2 = done("s", g.scalar.activation(T.v2[:], win.indirect(off(2)), FN.Identity))
-        g3 = done("s", g.scalar.activation(T.v3[:], win.indirect(off(3)), FN.Identity))
+        g2 = done("s", g.scalar.activation(val(2), win.indirect(off(2)), FN.Identity, scale=-1.0))
+        g3 = done("s", g.scalar.activation(val(3), win.indirect(off(3)), FN.Identity, scale=-1.0))
         need("p", [g2])
-        w2 = way_mm(T.psa, T.eye, T.v2, 0, K, False)
+        mm(T.psa[:, 0:512], T.eye, T.vall[:, 2 * K:2 * K + 512], False, True)
+        w2 = mm(T.psa[:, 512:K], T.eye, T.vall[:, 2 * K + 512:3 * K], False, True)
+        need("p", [g0])
+        v0 = values(0, T.psd, T.d0, b, c0)
         need("p", [g3])
-        wy = mm(T.psg[:, 0:Y], T.eye[:], T.v3[:, KY:K], False, True)
-        w3 = way_mm(T.psb, T.eye, T.v3, 0, KY, False)
+        wy = mm(psy, T.eye, T.vall[:, 3 * K + KY:4 * K], False, True)
+        mm(T.psb[:, 0:512], T.eye, T.vall[:, 3 * K:3 * K + 512], False, True)
+        w3 = mm(T.psb[:, 512:KY], T.eye, T.vall[:, 3 * K + 512:3 * K + KY], False, True)
+        need("p", [g1])
+        v1 = values(1, T.psf, T.d1, b, c0)
         need("v", [g0])
         done("v", g.vector.tensor_reduce(T.acc[:, 0:1], T.d0[:], X.X, A.add, apply_absolute_value=True))
         need("v", [wy])
-        ry = done("v", g.vector.tensor_reduce(T.accb[:, 3:4], T.psg[:, 0:Y], X.X, A.add, apply_absolute_value=True))
+        ry = done("v", g.vector.tensor_reduce(T.accb[:, 3:4], psy, X.X, A.add, apply_absolute_value=True))
         need("v", [g1])
         r1 = done("v", g.vector.tensor_reduce(T.acc[:, 1:2], T.d1[:], X.X, A.add, apply_absolute_value=True))
         need("s", [w2])
         a2 = done("s", g.scalar.activation(T.junk2[:], T.psa[:, 0:K], FN.Abs, accum_out=T.acc[:, 2:3]))
         need("s", [w3])
         a3 = done("s", g.scalar.activation(T.junk3[:], T.psb[:, 0:KY], FN.Abs, accum_out=T.acc[:, 3:4]))
+        need("s", [v0])
+        cs = done("s", g.scalar.activation(T.vall[:, 0:512], T.psd[:, 0:512], FN.Identity))
         need("p", [ry])
-        mm(T.psc[:, 0:O], T.blk[:], T.accb[:, 0:O], True, False)
+        mm(T.psc[:, 0:O], T.blk, T.accb[:, 0:O], True, False)
         need("p", [r1, a3])
-        el = mm(T.psc[:, 0:O], T.blk[:], T.acc[:, 0:O], False, True)
-        if t < NT - 1:
-            conv[t + 1] = convert(t + 1)
+        el = mm(T.psc[:, 0:O], T.blk, T.acc[:, 0:O], False, True)
+        need("v", [v1])
+        done("v", g.vector.tensor_copy(T.vall[:, 512:K], T.psg[:, 0:R]))
+        done("v", g.vector.tensor_copy(T.vall[:, K + 512:2 * K], T.psg[:, R:2 * R]))
+        done("v", g.vector.tensor_copy(T.vall[:, K:K + E], T.psf[:, 0:E]))
         need("v", [el])
         e1 = done("v", g.vector.tensor_tensor_scan(T.nmax[:, 0:O], T.psc[:, 0:O], T.low[:, 0:O], -1.0e9, A.max, A.max))
+        cv = done("v", g.vector.tensor_copy(T.vall[:, K + E:K + 512], T.psf[:, E:512]))
         need("s", [e1])
         e3 = done("s", g.scalar.activation(T.flag[:, 0:O - 1], T.nmax[:, 0:O - 1], FN.Sign, bias=T.nmax[:, O - 1:O], scale=-1.0,
                                            accum_out=T.wcol[:, 0:1]))
-        need("v", [e3, kbase])
-        e4 = done("v", g.vector.tensor_scalar(T.sel[:, 0:3], T.base[:, 0:3], T.wcol[:, 0:1], float(LC), A.add, A.mult))
-        need("v", [e4])
-        e5 = done("v", g.vector.tensor_copy(T.offw[:, 0:48], lw.indirect(T.sel[:, 0:3])))
+        need("p", [cs])
+        mm(T.psd[:, 0:HA - H1], T.eye, b[:, c0 + H1:c0 + HA], True, False)
+        need("p", [cv])
+        mm(T.psf[:, 0:K - HA], T.eye, b[:, c0 + HA:c0 + K], True, False)
+        need("v", [e3, kbase, kbv])
+        e4 = done("v", g.vector.tensor_scalar(T.selv[:, 0:LC], T.basev[:], T.wcol[:, 0:1], float(K), A.add, A.mult))
+        e5 = done("v", g.vector.tensor_scalar(T.sel[:, 0:3], T.base[:, 0:3], T.wcol[:, 0:1], float(LC), A.add, A.mult))
+        need("v", [e4, cs])
+        x1 = done("v", g.vector.tensor_tensor(T.dw[:], vwin.indirect(T.selv[:, 0:HC]), b[:, c0:c0 + H1], A.add))
         need("v", [e5])
-        x1 = done("v", g.vector.tensor_tensor(T.dh[:], win.indirect(T.offw[:, 0:HC]), b[:, c0:c0 + H1], A.subtract))
-        done("v", g.vector.tensor_copy(T.vw[:, 0:B1], win.indirect(T.offw[:, 0:VB])))
-        need("s", [e5])
-        s2 = done("s", g.scalar.activation(T.vw[:, H1:HA], win.indirect(T.offw[:, HC:HC + A1]), FN.Identity))
-        s3 = done("s", g.scalar.activation(T.vw[:, HA:K], win.indirect(T.offw[:, HC + A1:LC]), FN.Identity))
-        s1 = done("s", g.scalar.activation(T.vw[:, B1:H1], win.indirect(T.offw[:, VB:HC]), FN.Identity))
+        e6 = done("v", g.vector.tensor_copy(T.offw[:, 0:48], lw.indirect(T.sel[:, 0:3])))
+        need("s", [e4])
+        s2 = done("s", g.scalar.activation(T.vw[:, H1:HA], vwin.indirect(T.selv[:, HC:HC + A1]), FN.Identity, scale=-1.0))
+        s3 = done("s", g.scalar.activation(T.vw[:, HA:K], vwin.indirect(T.selv[:, HC + A1:LC]), FN.Identity, scale=-1.0))
+        s1 = done("s", g.scalar.activation(T.vw[:, 0:H1], vwin.indirect(T.selv[:, 0:HC]), FN.Identity, scale=-1.0))
         need("p", [s2])
-        x2 = mm(T.psd[:, 0:HA - H1], T.neye[:], T.vw[:, H1:HA], False, True)
+        x2 = mm(T.psd[:, 0:HA - H1], T.neye, T.vw[:, H1:HA], False, True)
         need("p", [s3])
-        x2b = mm(T.psf[:, 0:K - HA], T.neye[:], T.vw[:, HA:K], False, True)
+        x3 = mm(T.psf[:, 0:K - HA], T.neye, T.vw[:, HA:K], False, True)
         need("v", [x1])
-        x3 = done("v", g.vector.tensor_scalar(T.dc[:], T.dh[:], -1.0, float(C), A.mult, A.min))
+        y1 = done("v", g.vector.tensor_scalar(T.ew[:, 0:H1], T.dw[:], float(C), float(-C), A.min, A.max))
         need("v", [x2])
-        done("v", g.vector.tensor_scalar(T.ew[:, H1:HA], T.psd[:, 0:HA - H1], float(C), float(-C), A.min, A.max))
+        y2 = done("v", g.vector.tensor_scalar(T.ew[:, H1:HA], T.psd[:, 0:HA - H1], float(C), float(-C), A.min, A.max))
         need("v", [x3])
-        x4 = done("v", g.vector.tensor_scalar(T.ew[:, 0:H1], T.dc[:], float(-C), None, A.max))
-        need("v", [x2b])
-        x5 = done("v", g.vector.tensor_scalar(T.ew[:, HA:K], T.psf[:, 0:K - HA], float(C), float(-C), A.min, A.max))
-        need("v", [x4, x5, s1])
+        y3 = done("v", g.vector.tensor_scalar(T.ew[:, HA:K], T.psf[:, 0:K - HA], float(C), float(-C), A.min, A.max))
+        if t < NT - 1:
+            conv[t + 1] = convert(t + 1)
+        need("v", [e6, y1, y2, y3, s1])
         sc = done("v", g.vector.tensor_tensor(win.indirect(T.offw[:, 0:LC]), T.vw[:], T.ew[:], A.add))
         ready = [sc]
         if t < NT - 1:
-            lay(t + 1, [a2], [a3, ry], [x5])
+            lay(t + 1, [a2], [a3, e1], [y2], [y3])
 
     g.sync.wait_ge(T.sem.cv, count["cv"])
     g.sync.dma_start(T.y[:], T.ref[:]).then_inc(T.sem.yst, 16)

import numpy as np
from concourse.mybir import dt, AluOpType, AxisListType, ActivationFunctionType

N, W, K, F, O, C = 4, 4096, 640, 2, 4, 8
LC = K // 16
FC = O * LC
Y = 104
KY = K - Y
HC, A1 = 20, 12
H1, HA = 16 * HC, 16 * (HC + A1)
R = K - 512
E = 128

SCRATCH = {
    "ref": ("sbuf", [128, W], "bfloat16"),
    "obsb": ("sbuf", [128, N * F * K], "bfloat16"),
    "opsb": ("sbuf", [128, N * F * FC], "int32"),
    "lo1": ("sbuf", [128, F * K], "bfloat16"),
    "lo2": ("sbuf", [128, F * K], "bfloat16"),
    "lo3": ("sbuf", [128, F * K], "bfloat16"),
    "ll1": ("sbuf", [128, F * FC], "int32"),
    "ll2": ("sbuf", [128, F * FC], "int32"),
    "ll3": ("sbuf", [128, F * FC], "int32"),
    "offs": ("sbuf", [128, N * F * FC], "uint16"),
    "d0": ("sbuf", [128, K], "float16"),
    "d1": ("sbuf", [128, K], "float16"),
    "vall": ("sbuf", [128, O * K], "bfloat16"),
    "junk2": ("sbuf", [128, K], "float32"),
    "junk3": ("sbuf", [128, KY], "float32"),
    "acc": ("sbuf", [128, 8], "float32"),
    "accb": ("sbuf", [128, 8], "float32"),
    "nmax": ("sbuf", [128, 8], "float32"),
    "flag": ("sbuf", [128, 8], "float32"),
    "wcol": ("sbuf", [128, 8], "float32"),
    "low": ("sbuf", [128, 8], "float32"),
    "sel": ("sbuf", [128, 16], "uint16"),
    "selv": ("sbuf", [128, 48], "uint16"),
    "offw": ("sbuf", [128, 48], "uint16"),
    "dw": ("sbuf", [128, H1], "bfloat16"),
    "vw": ("sbuf", [128, K], "bfloat16"),
    "ew": ("sbuf", [128, K], "bfloat16"),
    "onesf": ("sbuf", [128, 128], "float32"),
    "blk0": ("sbuf", [128, 128], "float32"),
    "blk": ("sbuf", [128, 128], "float32"),
    "onesb": ("sbuf", [128, 128], "bfloat16"),
    "negb": ("sbuf", [128, 128], "bfloat16"),
    "eye": ("sbuf", [128, 128], "bfloat16"),
    "neye": ("sbuf", [128, 128], "bfloat16"),
    "neyeh": ("sbuf", [128, 128], "float16"),
    "ip": ("sbuf", [128, LC], "int32"),
    "ia": ("sbuf", [128, LC], "int32"),
    "ic": ("sbuf", [128, LC], "int32"),
    "bs": ("sbuf", [128, LC], "float32"),
    "bt": ("sbuf", [128, 4], "float32"),
    "base": ("sbuf", [128, 4], "float32"),
    "basev": ("sbuf", [128, LC], "float32"),
    "psa": ("psum", [128, 1024], "float32"),
    "psb": ("psum", [128, 1024], "float32"),
    "psc": ("psum", [128, 512], "float32"),
    "psd": ("psum", [128, 512], "float32"),
    "psf": ("psum", [128, 512], "float32"),
    "psg": ("psum", [128, 512], "float32"),
}
SEMAPHORES = ["cv", "cs", "cp", "cg", "lops0", "lops1", "lobs0", "lobs1", "lref", "lsend1", "lsend2", "lsend3",
              "llist1", "llist2", "llist3", "arr1", "arr2", "arr3", "sent", "yst"]


def rank_program(g, core, T, topo):
    q = T.rank_of(core)
    if q is None:
        return
    A, X, FN = AluOpType, AxisListType, ActivationFunctionType
    queue = {"v": g.vector, "s": g.scalar, "p": g.tensor, "g": g}
    count = {"cv": 0, "cs": 0, "cp": 0, "cg": 0}
    seen = {"v": {}, "s": {}, "p": {}, "g": {}}

    def need(e, deps):
        top = {}
        for name, n in deps:
            top[name] = max(top.get(name, 0), n)
        for name in top:
            if seen[e].get(name, 0) < top[name]:
                queue[e].wait_ge(T.sem[name], top[name])
                seen[e][name] = top[name]

    def done(e, inst):
        name = "c" + e
        inst.then_inc(T.sem[name], 1)
        count[name] += 1
        return (name, count[name])

    oc, bc = q * F * FC, q * F * K
    g.sync.dma_start(T.opsb[:, oc:oc + FC], T.ops[:, oc:oc + FC]).then_inc(T.sem.lops0, 16)
    g.scalar.dma_start(T.obsb[:, bc:bc + K], T.obs[:, bc:bc + K]).then_inc(T.sem.lobs0, 16)
    g.sync.dma_start(T.ref[:], T.ref0[:]).then_inc(T.sem.lref, 16)

    def load(d):
        o = (q - d) % N
        g.sync.dma_start(T.opsb[:, o * F * FC:(o + 1) * F * FC],
                         T.ops[:, o * F * FC:(o + 1) * F * FC]).then_inc(T.sem["llist%d" % d], 16)
        g.sync.dma_start(T.obsb[:, o * F * K:(o + 1) * F * K],
                         T.obs[:, o * F * K:(o + 1) * F * K]).then_inc(T.sem["lsend%d" % d], 16)

    load(1)
    g.sync.dma_start(T.opsb[:, oc + FC:oc + 2 * FC], T.ops[:, oc + FC:oc + 2 * FC]).then_inc(T.sem.lops1, 16)
    g.sync.dma_start(T.obsb[:, bc + K:bc + 2 * K], T.obs[:, bc + K:bc + 2 * K]).then_inc(T.sem.lobs1, 16)
    load(2)
    load(3)

    m1 = done("v", g.vector.memset(T.onesb[:], 1.0))
    m2 = done("v", g.vector.memset(T.negb[:], -1.0))
    m3 = done("v", g.vector.memset(T.onesf[:], -1.0))
    done("v", g.vector.memset(T.low[:], -1.0e9))
    mz = done("v", g.vector.memset(T.accb[:], 0.0))
    i1 = done("g", g.iota(T.ip[:], [[16, LC]], 0, 1))
    i2 = done("g", g.iota(T.ic[:], [[16, LC]], 0, 0))
    need("g", [m1])
    te = done("g", g.affine_select(T.eye[:], T.onesb[:], [[-1, 128]], A.is_equal, 0.0, 0, 1))
    need("g", [m2])
    tn = done("g", g.affine_select(T.neye[:], T.negb[:], [[-1, 128]], A.is_equal, 0.0, 0, 1))
    need("g", [m3])
    b0 = done("g", g.affine_select(T.blk0[:], T.onesf[:], [[-16, 8], [0, 16]], A.is_ge, 0.0, 0, 1))
    need("g", [b0])
    tb = done("g", g.affine_select(T.blk[:], T.blk0[:], [[16, 8], [0, 16]], A.is_ge, 0.0, 15, -1))
    need("v", [i1])
    k1 = done("v", g.vector.tensor_scalar(T.ia[:], T.ip[:], 15, None, A.bitwise_and))
    need("v", [k1, i2])
    k2 = done("v", g.vector.tensor_tensor(T.bs[:], T.ia[:], T.ic[:], A.add))
    need("v", [k2])
    k3 = done("v", g.vector.tensor_scalar(T.bt[:], T.bs[:, 0:4], float(LC - 1), 0.25, A.min, A.add))
    kbv = done("v", g.vector.tensor_scalar(T.basev[:], T.bs[:], 0.25, 1.0 / K, A.add, A.mult))
    need("v", [k3])
    kbase = done("v", g.vector.tensor_scalar(T.base[:], T.bt[:], 1.0 / LC, None, A.mult))
    need("v", [tn])
    th = done("v", g.vector.tensor_copy(T.neyeh[:], T.neye[:]))

    nsent = 0
    for d in range(1, N):
        o = (q - d) % N
        dst = T.cores[o]
        rid, pid, _ = topo.addr(dst)
        mask = topo.mask(core, dst)
        ne = len(topo.engines(core, dst))
        for land, src, sem in ((T["ll%d" % d], T.opsb[:, o * F * FC:(o + 1) * F * FC], T.sem["llist%d" % d]),
                               (T["lo%d" % d], T.obsb[:, o * F * K:(o + 1) * F * K], T.sem["lsend%d" % d])):
            g.wait_ge(sem, 16)
            g.remote_dma(land[:], src, T.sem["arr%d" % d], T.sem.sent, pid, rid, mask)
            nsent += ne

    def frame(t):
        d, f = t // F, t % F
        if d == 0:
            b = T.obsb
            c0 = bc + f * K
            dep = [("lobs%d" % f, 16)]
            ldep = [("lops%d" % f, 16)]
            lw = T.opsb[:, oc + f * FC:oc + (f + 1) * FC]
        else:
            b = T["lo%d" % d]
            c0 = f * K
            src = T.cores[(q + d) % N]
            dep = ldep = [("arr%d" % d, 2 * len(topo.engines(src, core)))]
            lw = T["ll%d" % d][:, f * FC:(f + 1) * FC]
        return b, c0, dep, lw, ldep

    def convert(t):
        _, _, _, lw, ldep = frame(t)
        need("v", ldep)
        return done("v", g.vector.tensor_copy(T.offs[:, t * FC:(t + 1) * FC], lw))

    def mm(out, lhsT, rhs, start, stop):
        return done("p", g.tensor.matmul(out, lhsT[:], rhs, start, stop))

    psy = T.psc[:, 128:128 + Y]

    def lay(t, free_a, free_b, free_d, free_f):
        b, c0, dep, _, _ = frame(t)
        need("p", dep + free_a)
        mm(T.psa[:, 0:512], T.eye, b[:, c0:c0 + 512], True, False)
        mm(T.psa[:, 512:K], T.eye, b[:, c0 + 512:c0 + K], True, False)
        need("p", free_d)
        mm(T.psd[:, 0:512], T.neye, b[:, c0:c0 + 512], True, False)
        need("p", free_b)
        mm(T.psb[:, 0:512], T.eye, b[:, c0:c0 + 512], True, False)
        mm(T.psb[:, 512:KY], T.eye, b[:, c0 + 512:c0 + KY], True, False)
        mm(psy, T.eye, b[:, c0 + KY:c0 + K], True, False)
        need("p", free_f)
        mm(T.psf[:, 0:512], T.neye, b[:, c0:c0 + 512], True, False)

    def values(o, ps, d, b, c0):
        mm(ps[:, 0:512], T.neyeh, d[:, 0:512], False, True)
        rest = T.psg[:, o * R:(o + 1) * R]
        mm(rest, T.neye, b[:, c0 + 512:c0 + K], True, False)
        return mm(rest, T.neyeh, d[:, 512:K], False, True)

    conv = {0: convert(0)}
    need("p", [te, tn])
    lay(0, [], [], [], [])
    need("p", [tb, mz, th])

    ready = [("lref", 16)]
    win = T.ref[:, 0:W]
    vwin = T.vall[:, 0:O * K]
    NT = N * F
    for t in range(NT):
        b, c0, dep, lw, _ = frame(t)
        off = lambda a: T.offs[:, t * FC + a * LC:t * FC + (a + 1) * LC]
        val = lambda a: T.vall[:, a * K:(a + 1) * K]
        need("v", ready + dep + [conv[t]])
        g0 = done("v", g.vector.tensor_tensor(T.d0[:], win.indirect(off(0)), b[:, c0:c0 + K], A.subtract))
        g1 = done("v", g.vector.tensor_tensor(T.d1[:], win.indirect(off(1)), b[:, c0:c0 + K], A.subtract))
        need("s", ready + [conv[t]])
        g2 = done("s", g.scalar.activation(val(2), win.indirect(off(2)), FN.Identity, scale=-1.0))
        g3 = done("s", g.scalar.activation(val(3), win.indirect(off(3)), FN.Identity, scale=-1.0))
        need("p", [g2])
        mm(T.psa[:, 0:512], T.eye, T.vall[:, 2 * K:2 * K + 512], False, True)
        w2 = mm(T.psa[:, 512:K], T.eye, T.vall[:, 2 * K + 512:3 * K], False, True)
        need("p", [g0])
        v0 = values(0, T.psd, T.d0, b, c0)
        need("p", [g3])
        wy = mm(psy, T.eye, T.vall[:, 3 * K + KY:4 * K], False, True)
        mm(T.psb[:, 0:512], T.eye, T.vall[:, 3 * K:3 * K + 512], False, True)
        w3 = mm(T.psb[:, 512:KY], T.eye, T.vall[:, 3 * K + 512:3 * K + KY], False, True)
        need("p", [g1])
        v1 = values(1, T.psf, T.d1, b, c0)
        need("v", [g0])
        done("v", g.vector.tensor_reduce(T.acc[:, 0:1], T.d0[:], X.X, A.add, apply_absolute_value=True))
        need("v", [wy])
        ry = done("v", g.vector.tensor_reduce(T.accb[:, 3:4], psy, X.X, A.add, apply_absolute_value=True))
        need("v", [g1])
        r1 = done("v", g.vector.tensor_reduce(T.acc[:, 1:2], T.d1[:], X.X, A.add, apply_absolute_value=True))
        need("s", [w2])
        a2 = done("s", g.scalar.activation(T.junk2[:], T.psa[:, 0:K], FN.Abs, accum_out=T.acc[:, 2:3]))
        need("s", [w3])
        a3 = done("s", g.scalar.activation(T.junk3[:], T.psb[:, 0:KY], FN.Abs, accum_out=T.acc[:, 3:4]))
        need("s", [v0])
        cs = done("s", g.scalar.activation(T.vall[:, 0:512], T.psd[:, 0:512], FN.Identity))
        need("p", [ry])
        mm(T.psc[:, 0:O], T.blk, T.accb[:, 0:O], True, False)
        need("p", [r1, a3])
        el = mm(T.psc[:, 0:O], T.blk, T.acc[:, 0:O], False, True)
        need("v", [v1])
        done("v", g.vector.tensor_copy(T.vall[:, 512:K], T.psg[:, 0:R]))
        done("v", g.vector.tensor_copy(T.vall[:, K + 512:2 * K], T.psg[:, R:2 * R]))
        done("v", g.vector.tensor_copy(T.vall[:, K:K + E], T.psf[:, 0:E]))
        need("v", [el])
        e1 = done("v", g.vector.tensor_tensor_scan(T.nmax[:, 0:O], T.psc[:, 0:O], T.low[:, 0:O], -1.0e9, A.max, A.max))
        cv = done("v", g.vector.tensor_copy(T.vall[:, K + E:K + 512], T.psf[:, E:512]))
        need("s", [e1])
        e3 = done("s", g.scalar.activation(T.flag[:, 0:O - 1], T.nmax[:, 0:O - 1], FN.Sign, bias=T.nmax[:, O - 1:O], scale=-1.0,
                                           accum_out=T.wcol[:, 0:1]))
        need("p", [cs])
        mm(T.psd[:, 0:HA - H1], T.eye, b[:, c0 + H1:c0 + HA], True, False)
        need("p", [cv])
        mm(T.psf[:, 0:K - HA], T.eye, b[:, c0 + HA:c0 + K], True, False)
        need("v", [e3, kbase, kbv])
        e4 = done("v", g.vector.tensor_scalar(T.selv[:, 0:LC], T.basev[:], T.wcol[:, 0:1], float(K), A.add, A.mult))
        e5 = done("v", g.vector.tensor_scalar(T.sel[:, 0:3], T.base[:, 0:3], T.wcol[:, 0:1], float(LC), A.add, A.mult))
        need("v", [e4, cs])
        x1 = done("v", g.vector.tensor_tensor(T.dw[:], vwin.indirect(T.selv[:, 0:HC]), b[:, c0:c0 + H1], A.add))
        need("v", [e5])
        e6 = done("v", g.vector.tensor_copy(T.offw[:, 0:48], lw.indirect(T.sel[:, 0:3])))
        need("s", [e4])
        s2 = done("s", g.scalar.activation(T.vw[:, H1:HA], vwin.indirect(T.selv[:, HC:HC + A1]), FN.Identity, scale=-1.0))
        s3 = done("s", g.scalar.activation(T.vw[:, HA:K], vwin.indirect(T.selv[:, HC + A1:LC]), FN.Identity, scale=-1.0))
        s1 = done("s", g.scalar.activation(T.vw[:, 0:H1], vwin.indirect(T.selv[:, 0:HC]), FN.Identity, scale=-1.0))
        need("p", [s2])
        x2 = mm(T.psd[:, 0:HA - H1], T.neye, T.vw[:, H1:HA], False, True)
        need("p", [s3])
        x3 = mm(T.psf[:, 0:K - HA], T.neye, T.vw[:, HA:K], False, True)
        need("v", [x1])
        y1 = done("v", g.vector.tensor_scalar(T.ew[:, 0:H1], T.dw[:], float(C), float(-C), A.min, A.max))
        need("v", [x2])
        y2 = done("v", g.vector.tensor_scalar(T.ew[:, H1:HA], T.psd[:, 0:HA - H1], float(C), float(-C), A.min, A.max))
        need("v", [x3])
        y3 = done("v", g.vector.tensor_scalar(T.ew[:, HA:K], T.psf[:, 0:K - HA], float(C), float(-C), A.min, A.max))
        if t < NT - 1:
            conv[t + 1] = convert(t + 1)
        need("v", [e6, y1, y2, y3, s1])
        sc = done("v", g.vector.tensor_tensor(win.indirect(T.offw[:, 0:LC]), T.vw[:], T.ew[:], A.add))
        ready = [sc]
        if t < NT - 1:
            lay(t + 1, [a2], [a3, e1], [y2], [y3])

    g.sync.wait_ge(T.sem.cv, count["cv"])
    g.sync.dma_start(T.y[:], T.ref[:]).then_inc(T.sem.yst, 16)
    g.sync.wait_ge(T.sem.yst, 16)
    g.wait_ge(T.sem.sent, nsent)
    need("g", [(c, count[c]) for c in ("cv", "cs", "cp", "cg")])
